import numpy as np
CORES = [33,38,57,62,81,86,161,166,185,190,209,214]
N = 12
T, M = 128, 256
def entries(a): return a.T.reshape(-1)
def pack(v, P): return np.ascontiguousarray(np.asarray(v, np.int32).reshape(-1, P).T)
def lists(rng, how):
    I = rng.integers(0, N * T, (N, 8, M))
    if how == "alike": I[:] = rng.integers(0, N * T, (N, 8, 1))
    if how == "same": I[:] = rng.integers(0, N * T, (N, 1, M))
    if how == "hotrank": I = T * int(rng.integers(N)) + rng.integers(0, T, (N, 8, M))
    if how == "own": I = T * np.arange(N).reshape(N, 1, 1) + rng.integers(0, T, (N, 8, M))
    if how == "edge": I = T * rng.integers(0, N, (N, 8, M)) + np.where(rng.random((N, 8, M)) < 0.5, 0, T - 1)
    return {"idx": np.stack([np.concatenate([pack(I[r, h], 16) for h in range(8)], axis=0) for r in range(N)])}
def setup_inputs(rng):
    return dict({"x": rng.standard_normal((N, 128, T), dtype=np.float32)}, **lists(rng, "uniform"))
def setup_inputs_alike(rng):
    d = setup_inputs(rng); d.update(lists(rng, "alike"))
    for k in ("x",): d[k] = (d[k].astype(np.float32) * 1048576.0).astype(d[k].dtype)
    return d
def setup_inputs_edge(rng):
    d = setup_inputs(rng); d.update(lists(rng, "edge"))
    for k in ("x",): d[k] = (d[k].astype(np.float32) * (1 / 1024.0)).astype(d[k].dtype)
    return d
def setup_inputs_hotrank(rng):
    d = setup_inputs(rng); d.update(lists(rng, "hotrank"))
    return d
def setup_inputs_own(rng):
    d = setup_inputs(rng); d.update(lists(rng, "own"))
    return d
def setup_inputs_same(rng):
    d = setup_inputs(rng); d.update(lists(rng, "same"))
    return d
def check_inputs(x):
    bad = []
    if x["idx"].min() < 0 or x["idx"].max() >= N * T: bad.append("idx out of range")
    return bad
def reference(x, idx):
    A = np.concatenate(list(x), axis=1)
    y = np.zeros((N, 128, M), x.dtype)
    for r in range(N):
        for h in range(8): y[r][16 * h:16 * h + 16] = A[16 * h:16 * h + 16][:, entries(idx[r][16 * h:16 * h + 16])]
    return {"y": y}

@@ -1,0 +1,166 @@
+from concourse.bass import DstId, RemoteDMATransfer
+
+N = 12
+W = 128
+M = 256
+NSIM = 256
+
+SCRATCH = {
+    "tab": ("sbuf", [128, N * W], "float32"),
+    "idxs": ("sbuf", [128, M // 16], "int32"),
+    "off": ("sbuf", [128, M // 16], "uint16"),
+    "yo": ("sbuf", [128, M], "float32"),
+}
+SEMAPHORES = ["xl", "il", "cv", "gd", "st", "ls"] + ["a%d" % k for k in range(N)]
+
+OPT = {
+    "groups": [2, 2, 1],
+    "nrelay": 2,
+    "last16": True,
+}
+
+_CACHE = {}
+
+
+def _bits(m):
+    return [b for b in range(16) if (m >> b) & 1]
+
+
+def _split(eng, n):
+    per = len(eng) // n
+    return [tuple(eng[j * per:(j + 1) * per]) for j in range(n)]
+
+
+def build_plan(cores, topo, opt):
+    key = lambda c: (topo.host(c), topo.chip(c))
+    chips = []
+    for c in cores:
+        if key(c) not in chips:
+            chips.append(key(c))
+    nch = len(chips)
+    members = [[c for c in cores if key(c) == k] for k in chips]
+    plan, passes, jobs = {}, {}, {}
+    used = set(cores)
+    for k, s in enumerate(cores):
+        ci = chips.index(key(s))
+        sib = [c for c in members[ci] if c != s][0]
+        relay, own, direct, need = [], [], [], []
+        for d in range(1, nch):
+            D = (ci + d) % nch
+            peer = [c for c in members[D] if topo.die(c) == topo.die(s)][0]
+            if topo.may_write(s, peer):
+                direct.append(peer)
+            else:
+                need.append((D, peer))
+        for i, (D, peer) in enumerate(need):
+            if i < opt["nrelay"]:
+                cand = [c for c in range(NSIM) if c not in used and topo.mates(c, peer)
+                        and topo.may_write(c, peer) and topo.may_write(s, c)]
+                load = lambda die: sum(1 for r, (kk, DD) in jobs.items()
+                                       if DD == D and topo.die(r) == die and key(r) != key(cores[kk]))
+                cand.sort(key=lambda c: (load(topo.die(c)), topo.die(c) != topo.die(s), c))
+                relay.append(cand[0])
+            else:
+                cand = [c for c in range(NSIM) if c not in used and key(c) == key(s) and topo.may_write(c, peer)]
+                cand.sort(key=lambda c: (topo.die(c) != topo.die(s), c))
+                own.append(cand[0])
+            used.add(cand[0])
+            jobs[cand[0]] = (k, D)
+        far = _bits(topo.mask(s, (relay + direct)[0]))
+        near = [b for b in _bits(topo.mask(s, sib)) if b not in far]
+        out = [(t, False) for t in relay] + [(t, True) for t in direct]
+        offc, pos = [], 0
+        for gi, size in enumerate(opt["groups"]):
+            grp = out[pos:pos + size]
+            pos += size
+            call = []
+            for (t, passon), eng in zip(grp, _split(far, max(1, len(grp)))):
+                call.append((k, t, eng))
+                if passon:
+                    passes.setdefault(t, []).append((gi, len(call), k))
+            offc.append(call)
+        onc = []
+        if own:
+            onc.append([(k, t, eng) for t, eng in zip(own, _split(near, len(own)))])
+        onc.append([(k, sib, tuple(near))])
+        calls = [offc[0]] + onc[:1]
+        rest_on = onc[1:]
+        for call in offc[1:]:
+            calls.append(call + (rest_on.pop(0) if rest_on else []))
+        calls += rest_on
+        plan[s] = [c for c in calls if c]
+    for r, (k, D) in jobs.items():
+        eng = _bits(topo.mask(r, members[D][0]))
+        plan[r] = [[(k, c, e) for c, e in zip(members[D], _split(eng, len(members[D])))]]
+    for c, lst in passes.items():
+        lst.sort()
+        sib = [x for x in members[chips.index(key(c))] if x != c][0]
+        every = _bits(topo.mask(c, sib))
+        far = _bits(topo.mask(c, [x for x in cores if key(x) != key(c) and topo.may_write(c, x)][0]))
+        near = [b for b in every if b not in far]
+        gis = sorted(set(gi for gi, _, _ in lst))
+        for gi in gis:
+            ps = [p for g_, _, p in lst if g_ == gi]
+            eng = every if (gi == gis[-1] and opt["last16"]) else near
+            plan[c].append([(p, sib, e) for p, e in zip(ps, _split(eng, len(ps)))])
+    return plan
+
+
+def rank_program(g, core, T, topo):
+    cores = [int(c) for c in T.cores]
+    if "plan" not in _CACHE:
+        _CACHE["plan"] = build_plan(cores, topo, OPT)
+    plan = _CACHE["plan"]
+    rank = T.rank_of(core)
+    if core not in plan:
+        return
+    sem = T.sem
+    lands = {}
+    for calls in plan.values():
+        for call in calls:
+            for p, d, eng in call:
+                if d == core:
+                    lands[p] = len(eng)
+    piece = lambda p: T.tab[:, p * W:(p + 1) * W]
+
+    if rank is not None:
+        g.sync.dma_start(piece(rank), T.x[:]).then_inc(sem.xl, 16)
+        g.scalar.dma_start(T.idxs[:], T.idx[:]).then_inc(sem.il, 16)
+        g.wait_ge(sem.xl, 16)
+
+    have, left = {rank}, 0
+    for call in plan[core]:
+        for p, d, eng in call:
+            if p not in have:
+                g.wait_ge(sem["a%d" % p], lands[p])
+                have.add(p)
+        trs = []
+        for p, d, eng in call:
+            rid, pid = topo.addr(d, core)
+            mask = sum(1 << b for b in eng)
+            left += len(eng)
+            trs.append((p, rid, pid, mask))
+        if len(trs) == 1:
+            p, rid, pid, mask = trs[0]
+            g.remote_dma(piece(p), piece(p), sem["a%d" % p], sem.ls, pid, rid, mask)
+        else:
+            g.remote_dma_fused(
+                [RemoteDMATransfer(dst_ids=[DstId(rid=rid, pnc=pid)], dma_engine_mask=mask, remote_sem=sem["a%d" % p],
+                                   src=piece(p), dst=piece(p)) for p, rid, pid, mask in trs],
+                local_sem=sem.ls)
+
+    if rank is not None:
+        v = g.vector
+        v.wait_ge(sem.il, 16)
+        v.tensor_copy(T.off[:], T.idxs[:]).then_inc(sem.cv, 1)
+        v.wait_ge(sem.cv, 1)
+        v.wait_ge(sem.xl, 16)
+        for p in range(N):
+            if p != rank:
+                v.wait_ge(sem["a%d" % p], lands[p])
+        v.tensor_copy(T.yo[:], T.tab[:, 0:N * W].indirect(T.off[:, 0:M // 16])).then_inc(sem.gd, 1)
+        g.sync.wait_ge(sem.gd, 1)
+        g.sync.dma_start(T.y[:], T.yo[:]).then_inc(sem.st, 16)
+        g.sync.wait_ge(sem.st, 16)
+
+    g.wait_ge(sem.ls, left)

@@ -1,22 +1,25 @@
 from concourse.bass import DstId, RemoteDMATransfer
+from concourse.mybir import ActivationFunctionType
 
 N = 12
 W = 128
 M = 256
 NSIM = 256
+P1 = 16
 
 SCRATCH = {
     "tab": ("sbuf", [128, N * W], "float32"),
+    "d1": ("dram", [128, P1], "float32"),
+    "d2": ("dram", [128, W - P1], "float32"),
     "idxs": ("sbuf", [128, M // 16], "int32"),
     "off": ("sbuf", [128, M // 16], "uint16"),
     "yo": ("sbuf", [128, M], "float32"),
 }
-SEMAPHORES = ["xl", "il", "cv", "gd", "st", "ls"] + ["a%d" % k for k in range(N)]
+SEMAPHORES = (["xl", "s1", "s2", "il", "cv", "gd", "st", "ls"] + ["a%d" % k for k in range(N)]
+              + ["b%d" % k for k in range(N)])
 
 OPT = {
-    "groups": [2, 2, 1],
-    "nrelay": 2,
-    "last16": True,
+    "cap": 4,
 }
 
 _CACHE = {}
@@ -41,68 +44,78 @@ def build_plan(cores, topo, opt):
     members = [[c for c in cores if key(c) == k] for k in chips]
     plan, passes, jobs = {}, {}, {}
     used = set(cores)
+    swin, brel = {}, {}
+    for s in cores:
+        for D in range(nch):
+            if topo.same_plane(s, members[D][0]):
+                swin[(D, topo.die(s))] = swin.get((D, topo.die(s)), 0) + 1
     for k, s in enumerate(cores):
         ci = chips.index(key(s))
         sib = [c for c in members[ci] if c != s][0]
-        relay, own, direct, need = [], [], [], []
+        relay, own, direct = [], [], []
         for d in range(1, nch):
             D = (ci + d) % nch
             peer = [c for c in members[D] if topo.die(c) == topo.die(s)][0]
-            if topo.may_write(s, peer):
+            if topo.same_plane(s, peer):
                 direct.append(peer)
+                continue
+            helpers = [c for c in range(NSIM) if c not in used and key(c) == key(s) and topo.may_write(c, peer)]
+            helpers.sort(key=lambda c: (topo.die(c) != topo.die(s), c))
+            if topo.may_write(s, peer):
+                if topo.host(s) != topo.host(peer) or brel.get(D):
+                    direct.append(peer)
+                    swin[(D, topo.die(s))] = swin.get((D, topo.die(s)), 0) + 1
+                    continue
+                brel[D] = 1
+                home = False
             else:
-                need.append((D, peer))
-        for i, (D, peer) in enumerate(need):
-            if i < opt["nrelay"]:
+                home = (topo.host(s) == topo.host(peer)
+                        and swin.get((D, topo.die(helpers[0])), 0) + len(members[D]) <= opt["cap"])
+            if home:
+                v = helpers[0]
+                swin[(D, topo.die(v))] = swin.get((D, topo.die(v)), 0) + len(members[D])
+                own.append(v)
+            else:
                 cand = [c for c in range(NSIM) if c not in used and topo.mates(c, peer)
                         and topo.may_write(c, peer) and topo.may_write(s, c)]
                 load = lambda die: sum(1 for r, (kk, DD) in jobs.items()
                                        if DD == D and topo.die(r) == die and key(r) != key(cores[kk]))
                 cand.sort(key=lambda c: (load(topo.die(c)), topo.die(c) != topo.die(s), c))
-                relay.append(cand[0])
-            else:
-                cand = [c for c in range(NSIM) if c not in used and key(c) == key(s) and topo.may_write(c, peer)]
-                cand.sort(key=lambda c: (topo.die(c) != topo.die(s), c))
-                own.append(cand[0])
-            used.add(cand[0])
-            jobs[cand[0]] = (k, D)
-        far = _bits(topo.mask(s, (relay + direct)[0]))
+                v = cand[0]
+                relay.append(v)
+            used.add(v)
+            jobs[v] = (k, D)
+        far = _bits(topo.mask(s, direct[0]))
         near = [b for b in _bits(topo.mask(s, sib)) if b not in far]
-        out = [(t, False) for t in relay] + [(t, True) for t in direct]
-        offc, pos = [], 0
-        for gi, size in enumerate(opt["groups"]):
-            grp = out[pos:pos + size]
-            pos += size
-            call = []
-            for (t, passon), eng in zip(grp, _split(far, max(1, len(grp)))):
-                call.append((k, t, eng))
-                if passon:
-                    passes.setdefault(t, []).append((gi, len(call), k))
-            offc.append(call)
-        onc = []
-        if own:
-            onc.append([(k, t, eng) for t, eng in zip(own, _split(near, len(own)))])
-        onc.append([(k, sib, tuple(near))])
-        calls = [offc[0]] + onc[:1]
-        rest_on = onc[1:]
-        for call in offc[1:]:
-            calls.append(call + (rest_on.pop(0) if rest_on else []))
-        calls += rest_on
-        plan[s] = [c for c in calls if c]
+        fused = lambda ts, eng, part: [(k, t, e, part) for t, e in zip(ts, _split(eng, max(1, len(ts))))]
+        calls = []
+        if relay or own:
+            calls.append(fused(relay, far, 1) + fused(own, near, 1))
+            calls.append(fused(relay[:2], far, 2) + fused(own, near, 2))
+            if relay[2:]:
+                calls.append(fused(relay[2:], far, 2))
+        first, pos = len(calls), len(relay)
+        while direct:
+            grp, direct = direct[:2], direct[2:]
+            calls.append(fused(grp, far, 0))
+            pos += len(grp)
+            for j, t in enumerate(grp):
+                passes.setdefault(t, []).append((pos, j, k))
+        calls[first if first else min(1, len(calls) - 1)] += fused([sib], near, 0)
+        plan[s] = calls
     for r, (k, D) in jobs.items():
         eng = _bits(topo.mask(r, members[D][0]))
-        plan[r] = [[(k, c, e) for c, e in zip(members[D], _split(eng, len(members[D])))]]
+        plan[r] = [[(k, c, e, part) for c, e in zip(members[D], _split(eng, len(members[D])))] for part in (1, 2)]
     for c, lst in passes.items():
         lst.sort()
         sib = [x for x in members[chips.index(key(c))] if x != c][0]
         every = _bits(topo.mask(c, sib))
         far = _bits(topo.mask(c, [x for x in cores if key(x) != key(c) and topo.may_write(c, x)][0]))
         near = [b for b in every if b not in far]
-        gis = sorted(set(gi for gi, _, _ in lst))
-        for gi in gis:
-            ps = [p for g_, _, p in lst if g_ == gi]
-            eng = every if (gi == gis[-1] and opt["last16"]) else near
-            plan[c].append([(p, sib, e) for p, e in zip(ps, _split(eng, len(ps)))])
+        ps = [p for _, _, p in lst]
+        while ps:
+            grp, ps = ps[:2], ps[2:]
+            plan[c].append([(p, sib, e, 0) for p, e in zip(grp, _split(near if ps else every, len(grp)))])
     return plan
 
 
@@ -118,48 +131,62 @@ def rank_program(g, core, T, topo):
     lands = {}
     for calls in plan.values():
         for call in calls:
-            for p, d, eng in call:
+            for p, d, eng, part in call:
                 if d == core:
-                    lands[p] = len(eng)
-    piece = lambda p: T.tab[:, p * W:(p + 1) * W]
+                    lands[(p, part)] = len(eng)
+    cols = {0: (0, W), 1: (0, P1), 2: (P1, W)}
+    piece = lambda p, part: T.tab[:, p * W + cols[part][0]:p * W + cols[part][1]]
+    stage = {1: T.d1, 2: T.d2}
+    src_ap = lambda p, part: stage[part][:] if part else piece(p, 0)
+    dst_ap = lambda p, d, part: piece(p, part) if d in cores else stage[part][:]
+    sname = lambda p, part: ("b%d" if part == 1 else "a%d") % p
+    loaded = {0: sem.xl, 1: sem.s1, 2: sem.s2}
 
     if rank is not None:
-        g.sync.dma_start(piece(rank), T.x[:]).then_inc(sem.xl, 16)
+        if any(part for call in plan[core] for _, _, _, part in call):
+            g.sync.dma_start(T.d1[:], T.x[:, 0:P1]).then_inc(sem.s1, 16)
+            g.scalar.dma_start(T.d2[:], T.x[:, P1:W]).then_inc(sem.s2, 16)
+        g.sync.dma_start(piece(rank, 0), T.x[:]).then_inc(sem.xl, 16)
         g.scalar.dma_start(T.idxs[:], T.idx[:]).then_inc(sem.il, 16)
-        g.wait_ge(sem.xl, 16)
 
-    have, left = {rank}, 0
+    have, left = set(), 0
     for call in plan[core]:
-        for p, d, eng in call:
-            if p not in have:
-                g.wait_ge(sem["a%d" % p], lands[p])
-                have.add(p)
+        for p, d, eng, part in call:
+            if (p, part) not in have:
+                if p == rank:
+                    g.wait_ge(loaded[part], 16)
+                else:
+                    g.wait_ge(sem[sname(p, part)], lands[(p, part)])
+                have.add((p, part))
         trs = []
-        for p, d, eng in call:
+        for p, d, eng, part in call:
             rid, pid = topo.addr(d, core)
             mask = sum(1 << b for b in eng)
             left += len(eng)
-            trs.append((p, rid, pid, mask))
+            trs.append((p, d, part, rid, pid, mask))
         if len(trs) == 1:
-            p, rid, pid, mask = trs[0]
-            g.remote_dma(piece(p), piece(p), sem["a%d" % p], sem.ls, pid, rid, mask)
+            p, d, part, rid, pid, mask = trs[0]
+            g.remote_dma(dst_ap(p, d, part), src_ap(p, part), sem[sname(p, part)], sem.ls, pid, rid, mask)
         else:
             g.remote_dma_fused(
-                [RemoteDMATransfer(dst_ids=[DstId(rid=rid, pnc=pid)], dma_engine_mask=mask, remote_sem=sem["a%d" % p],
-                                   src=piece(p), dst=piece(p)) for p, rid, pid, mask in trs],
+                [RemoteDMATransfer(dst_ids=[DstId(rid=rid, pnc=pid)], dma_engine_mask=mask, remote_sem=sem[sname(p, part)],
+                                   src=src_ap(p, part), dst=dst_ap(p, d, part)) for p, d, part, rid, pid, mask in trs],
                 local_sem=sem.ls)
 
     if rank is not None:
-        v = g.vector
+        v, s = g.vector, g.scalar
+        K = M // 16
         v.wait_ge(sem.il, 16)
         v.tensor_copy(T.off[:], T.idxs[:]).then_inc(sem.cv, 1)
-        v.wait_ge(sem.cv, 1)
-        v.wait_ge(sem.xl, 16)
-        for p in range(N):
-            if p != rank:
-                v.wait_ge(sem["a%d" % p], lands[p])
-        v.tensor_copy(T.yo[:], T.tab[:, 0:N * W].indirect(T.off[:, 0:M // 16])).then_inc(sem.gd, 1)
-        g.sync.wait_ge(sem.gd, 1)
+        for q in (v, s):
+            q.wait_ge(sem.cv, 1)
+            q.wait_ge(sem.xl, 16)
+            for (p, part) in sorted(lands):
+                q.wait_ge(sem[sname(p, part)], lands[(p, part)])
+        v.tensor_copy(T.yo[:, 0:M // 2], T.tab[:, 0:N * W].indirect(T.off[:, 0:K // 2])).then_inc(sem.gd, 1)
+        s.activation(T.yo[:, M // 2:M], T.tab[:, 0:N * W].indirect(T.off[:, K // 2:K]),
+                     ActivationFunctionType.Copy).then_inc(sem.gd, 1)
+        g.sync.wait_ge(sem.gd, 2)
         g.sync.dma_start(T.y[:], T.yo[:]).then_inc(sem.st, 16)
         g.sync.wait_ge(sem.st, 16)
 

from concourse.bass import DstId, RemoteDMATransfer
from concourse.mybir import ActivationFunctionType

N = 12
W = 128
M = 256
NSIM = 256
P1 = 16

SCRATCH = {
    "tab": ("sbuf", [128, N * W], "float32"),
    "d1": ("dram", [128, P1], "float32"),
    "d2": ("dram", [128, W - P1], "float32"),
    "idxs": ("sbuf", [128, M // 16], "int32"),
    "off": ("sbuf", [128, M // 16], "uint16"),
    "yo": ("sbuf", [128, M], "float32"),
}
SEMAPHORES = (["xl", "s1", "s2", "il", "cv", "gd", "st", "ls"] + ["a%d" % k for k in range(N)]
              + ["b%d" % k for k in range(N)])

OPT = {
    "cap": 4,
}

_CACHE = {}


def _bits(m):
    return [b for b in range(16) if (m >> b) & 1]


def _split(eng, n):
    per = len(eng) // n
    return [tuple(eng[j * per:(j + 1) * per]) for j in range(n)]


def build_plan(cores, topo, opt):
    key = lambda c: (topo.host(c), topo.chip(c))
    chips = []
    for c in cores:
        if key(c) not in chips:
            chips.append(key(c))
    nch = len(chips)
    members = [[c for c in cores if key(c) == k] for k in chips]
    plan, passes, jobs = {}, {}, {}
    used = set(cores)
    swin, brel = {}, {}
    for s in cores:
        for D in range(nch):
            if topo.same_plane(s, members[D][0]):
                swin[(D, topo.die(s))] = swin.get((D, topo.die(s)), 0) + 1
    for k, s in enumerate(cores):
        ci = chips.index(key(s))
        sib = [c for c in members[ci] if c != s][0]
        relay, own, direct = [], [], []
        for d in range(1, nch):
            D = (ci + d) % nch
            peer = [c for c in members[D] if topo.die(c) == topo.die(s)][0]
            if topo.same_plane(s, peer):
                direct.append(peer)
                continue
            helpers = [c for c in range(NSIM) if c not in used and key(c) == key(s) and topo.may_write(c, peer)]
            helpers.sort(key=lambda c: (topo.die(c) != topo.die(s), c))
            if topo.may_write(s, peer):
                if topo.host(s) != topo.host(peer) or brel.get(D):
                    direct.append(peer)
                    swin[(D, topo.die(s))] = swin.get((D, topo.die(s)), 0) + 1
                    continue
                brel[D] = 1
                home = False
            else:
                home = (topo.host(s) == topo.host(peer)
                        and swin.get((D, topo.die(helpers[0])), 0) + len(members[D]) <= opt["cap"])
            if home:
                v = helpers[0]
                swin[(D, topo.die(v))] = swin.get((D, topo.die(v)), 0) + len(members[D])
                own.append(v)
            else:
                cand = [c for c in range(NSIM) if c not in used and topo.mates(c, peer)
                        and topo.may_write(c, peer) and topo.may_write(s, c)]
                load = lambda die: sum(1 for r, (kk, DD) in jobs.items()
                                       if DD == D and topo.die(r) == die and key(r) != key(cores[kk]))
                cand.sort(key=lambda c: (load(topo.die(c)), topo.die(c) != topo.die(s), c))
                v = cand[0]
                relay.append(v)
            used.add(v)
            jobs[v] = (k, D)
        far = _bits(topo.mask(s, direct[0]))
        near = [b for b in _bits(topo.mask(s, sib)) if b not in far]
        fused = lambda ts, eng, part: [(k, t, e, part) for t, e in zip(ts, _split(eng, max(1, len(ts))))]
        calls = []
        if relay or own:
            calls.append(fused(relay, far, 1) + fused(own, near, 1))
            calls.append(fused(relay[:2], far, 2) + fused(own, near, 2))
            if relay[2:]:
                calls.append(fused(relay[2:], far, 2))
        first, pos = len(calls), len(relay)
        while direct:
            grp, direct = direct[:2], direct[2:]
            calls.append(fused(grp, far, 0))
            pos += len(grp)
            for j, t in enumerate(grp):
                passes.setdefault(t, []).append((pos, j, k))
        calls[first if first else min(1, len(calls) - 1)] += fused([sib], near, 0)
        plan[s] = calls
    for r, (k, D) in jobs.items():
        eng = _bits(topo.mask(r, members[D][0]))
        plan[r] = [[(k, c, e, part) for c, e in zip(members[D], _split(eng, len(members[D])))] for part in (1, 2)]
    for c, lst in passes.items():
        lst.sort()
        sib = [x for x in members[chips.index(key(c))] if x != c][0]
        every = _bits(topo.mask(c, sib))
        far = _bits(topo.mask(c, [x for x in cores if key(x) != key(c) and topo.may_write(c, x)][0]))
        near = [b for b in every if b not in far]
        ps = [p for _, _, p in lst]
        while ps:
            grp, ps = ps[:2], ps[2:]
            plan[c].append([(p, sib, e, 0) for p, e in zip(grp, _split(near if ps else every, len(grp)))])
    return plan


def rank_program(g, core, T, topo):
    cores = [int(c) for c in T.cores]
    if "plan" not in _CACHE:
        _CACHE["plan"] = build_plan(cores, topo, OPT)
    plan = _CACHE["plan"]
    rank = T.rank_of(core)
    if core not in plan:
        return
    sem = T.sem
    lands = {}
    for calls in plan.values():
        for call in calls:
            for p, d, eng, part in call:
                if d == core:
                    lands[(p, part)] = len(eng)
    cols = {0: (0, W), 1: (0, P1), 2: (P1, W)}
    piece = lambda p, part: T.tab[:, p * W + cols[part][0]:p * W + cols[part][1]]
    stage = {1: T.d1, 2: T.d2}
    src_ap = lambda p, part: stage[part][:] if part else piece(p, 0)
    dst_ap = lambda p, d, part: piece(p, part) if d in cores else stage[part][:]
    sname = lambda p, part: ("b%d" if part == 1 else "a%d") % p
    loaded = {0: sem.xl, 1: sem.s1, 2: sem.s2}

    if rank is not None:
        if any(part for call in plan[core] for _, _, _, part in call):
            g.sync.dma_start(T.d1[:], T.x[:, 0:P1]).then_inc(sem.s1, 16)
            g.scalar.dma_start(T.d2[:], T.x[:, P1:W]).then_inc(sem.s2, 16)
        g.sync.dma_start(piece(rank, 0), T.x[:]).then_inc(sem.xl, 16)
        g.scalar.dma_start(T.idxs[:], T.idx[:]).then_inc(sem.il, 16)

    have, left = set(), 0
    for call in plan[core]:
        for p, d, eng, part in call:
            if (p, part) not in have:
                if p == rank:
                    g.wait_ge(loaded[part], 16)
                else:
                    g.wait_ge(sem[sname(p, part)], lands[(p, part)])
                have.add((p, part))
        trs = []
        for p, d, eng, part in call:
            rid, pid = topo.addr(d, core)
            mask = sum(1 << b for b in eng)
            left += len(eng)
            trs.append((p, d, part, rid, pid, mask))
        if len(trs) == 1:
            p, d, part, rid, pid, mask = trs[0]
            g.remote_dma(dst_ap(p, d, part), src_ap(p, part), sem[sname(p, part)], sem.ls, pid, rid, mask)
        else:
            g.remote_dma_fused(
                [RemoteDMATransfer(dst_ids=[DstId(rid=rid, pnc=pid)], dma_engine_mask=mask, remote_sem=sem[sname(p, part)],
                                   src=src_ap(p, part), dst=dst_ap(p, d, part)) for p, d, part, rid, pid, mask in trs],
                local_sem=sem.ls)

    if rank is not None:
        v, s = g.vector, g.scalar
        K = M // 16
        v.wait_ge(sem.il, 16)
        v.tensor_copy(T.off[:], T.idxs[:]).then_inc(sem.cv, 1)
        for q in (v, s):
            q.wait_ge(sem.cv, 1)
            q.wait_ge(sem.xl, 16)
            for (p, part) in sorted(lands):
                q.wait_ge(sem[sname(p, part)], lands[(p, part)])
        v.tensor_copy(T.yo[:, 0:M // 2], T.tab[:, 0:N * W].indirect(T.off[:, 0:K // 2])).then_inc(sem.gd, 1)
        s.activation(T.yo[:, M // 2:M], T.tab[:, 0:N * W].indirect(T.off[:, K // 2:K]),
                     ActivationFunctionType.Copy).then_inc(sem.gd, 1)
        g.sync.wait_ge(sem.gd, 2)
        g.sync.dma_start(T.y[:], T.yo[:]).then_inc(sem.st, 16)
        g.sync.wait_ge(sem.st, 16)

    g.wait_ge(sem.ls, left)
